import numpy as np
import ml_dtypes


def mxq(x, axis, fmt="e4m3"):
    dtype, down = {"e4m3": (ml_dtypes.float8_e4m3fn, 7), "e5m2": (ml_dtypes.float8_e5m2, 14)}[fmt]
    v = np.moveaxis(np.asarray(x, np.float32).astype(ml_dtypes.bfloat16).astype(np.float64), axis, -1)
    blocks = v.reshape(v.shape[:-1] + (-1, 32))
    amax = np.abs(blocks).max(-1, keepdims=True)
    byte = np.maximum(np.where(amax > 0, np.frexp(amax)[1] - 1 + 127, 0) - down, 1)
    scale = np.exp2(byte - 127.0)
    codes = (blocks / scale).astype(np.float32).astype(dtype).astype(np.float64)
    return np.moveaxis((codes * scale).reshape(v.shape), -1, axis)


WIDE = False


def mx_kscale(k):
    if not WIDE:
        return np.ones(k)
    levels = np.array([10, -10, 5, -5, 0])
    if k % 512:
        return np.exp2(np.random.permutation(np.resize(levels, k // 32))).repeat(32)
    a = np.empty((k // 512, 16))
    for p in range(k // 512):
        a[p, :8] = np.random.permutation(np.resize(levels, 8))
        for g in range(8):
            far = levels[np.abs(levels - a[p, g]) >= 10]
            a[p, g + 8] = far[np.random.randint(len(far))]
    return np.exp2(a.ravel()).repeat(32)


def f64(x):
    return np.asarray(x).astype(np.float64)


def striped(idx):
    return np.tile(idx.reshape(-1, 16).T, (8, 1)).astype(np.uint16)


def unstriped(offs):
    return offs[:16].T.reshape(-1).astype(np.int64)


def striped8(idx):
    return np.concatenate([x.reshape(-1, 16).T for x in idx]).astype(np.uint16)


def runs(offs, k):
    lists = np.stack([offs[16 * r : 16 * r + 16].T.reshape(-1) for r in range(8)]).astype(np.int64)
    return lists[np.arange(k) % 512 // 64]


def pack_weight(w):
    k, n = w.shape
    w = f64(np.asarray(w, np.float32).astype(ml_dtypes.bfloat16)).reshape(k // 32, 32, n)
    amax = np.abs(w).max(1)
    byte = np.clip(np.where(amax > 0, np.frexp(amax)[1] - 1 + 127 - 7, 1), 1, 254)
    scaled = (w * np.exp2(127.0 - byte)[:, None, :]).reshape(k, n).astype(np.float32)
    words = np.ascontiguousarray(scaled.reshape(k // 512, 128, 4, n).transpose(0, 1, 3, 2)).astype(ml_dtypes.float8_e4m3fn).view(np.uint8)
    return words, np.ascontiguousarray(byte.astype(np.uint8).reshape(k // 512, 16, n))


def unpack_weight(words, scales):
    g, p, n, _ = words.shape
    vals = np.ascontiguousarray(words).view(ml_dtypes.float8_e4m3fn).astype(np.float64) * np.repeat(np.exp2(scales.astype(np.float64) - 127.0), 8, axis=1)[..., None]
    return vals.transpose(0, 1, 3, 2).reshape(g * 512, n)


def sigmoid(v):
    return 1.0 / (1.0 + np.exp(-np.maximum(v, -700.0)))

def planes(y):
    n, m = y.shape
    v = y.astype(np.float32).astype(ml_dtypes.bfloat16).astype(np.float64).reshape(n // 32, 32, m)
    top = np.abs(v).max(1)
    byte = np.clip(np.where(top > 0, np.frexp(top)[1] - 1 + 127 - 7, 1), 1, 254)
    codes = (v * np.exp2(127.0 - byte)[:, None, :]).reshape(n, m).astype(np.float32).astype(ml_dtypes.float8_e4m3fn).view(np.uint8)
    words = codes.reshape(n // 512, 128, 4, m).transpose(0, 1, 3, 2)
    return np.ascontiguousarray(words), np.ascontiguousarray(byte.astype(np.uint8).reshape(n // 512, 16, m))


K, T, S, H, W, C = 512, 2048, 512, 512, 2048, 512


def setup_inputs():
    n = np.random.standard_normal
    s = mx_kscale(K)[:, None]
    packed_xT = pack_weight(n((K, T)) * s)
    packed_w1 = pack_weight(n((K, H)) / np.sqrt(K) / s)
    return {
        "x_words": packed_xT[0],
        "x_scales": packed_xT[1],
        "w1_words": packed_w1[0],
        "w1_scales": packed_w1[1],
        "sl": np.random.uniform(1.5, 3.0, (H, 1)).astype(np.float32),
        "th": (0.5 * n((H, 1))).astype(np.float32),
        "gs": (np.random.uniform(0.5, 1.5, (K, 1)) / s).astype(np.float32),
        "sl2": np.random.uniform(1.0, 2.0, (C, 1)).astype(np.float32),
        "th2": (0.5 * n((C, 1))).astype(np.float32),
        "offs": striped(np.random.permutation(T)[:S]),
        "n1": striped(np.random.randint(0, S, W)),
        "ca": striped(np.random.permutation(T)[:C]),
        "cb": striped(np.random.permutation(T)[:C]),
        "cd": striped(np.random.permutation(T)[:C]),
        "n2": striped8(np.stack([np.random.permutation(S) for _ in range(8)])),
        "n3": striped8(np.stack([np.random.permutation(S) for _ in range(8)])),
        "n4": striped(np.random.permutation(S)),
        "n5": striped(np.random.permutation(S)),
    }


def reference(x_words, x_scales, w1_words, w1_scales, sl, th, gs, sl2, th2, offs, n1, ca, cb, cd, n2, n3, n4, n5):
    x_ca = unpack_weight(x_words, x_scales)[:, unstriped(ca)]
    xq = unpack_weight(x_words, x_scales)[:, unstriped(offs)]
    y = unpack_weight(w1_words, w1_scales).T @ xq
    sg = sigmoid(f64(sl) * (y[:, unstriped(n1)] - f64(th)))
    cnt = sg.reshape(H, S, 4).sum(axis=2)
    z = f64(gs) * np.maximum(y, cnt + -1.5)
    zq = mxq(z, 0, "e4m3")
    a = 0.0625 * (x_ca.T @ zq)
    x_cb = unpack_weight(x_words, x_scales)[:, unstriped(cb)]
    b = 0.0625 * (x_cb.T @ zq)
    sg2 = sigmoid(f64(sl2) * (b[np.arange(C)[:, None], runs(n2, C)] - f64(th2)))
    m1 = a * sg2 - (0.5 * (a[np.arange(C)[:, None], runs(n3, C)]))
    x_cd = unpack_weight(x_words, x_scales)[:, unstriped(cd)]
    q = 0.0625 * (x_cd.T @ zq)
    out_0 = np.maximum(m1, q[:, unstriped(n5)]) - (np.minimum(m1[:, unstriped(n4)], q))
    return (out_0,) + planes(out_0)

@@ -1,0 +1,273 @@
+from contextlib import ExitStack
+
+import concourse.mybir as mybir
+
+F32 = mybir.dt.float32
+BF16 = mybir.dt.bfloat16
+I32 = mybir.dt.int32
+U32 = mybir.dt.uint32
+U16 = mybir.dt.uint16
+U8 = mybir.dt.uint8
+FP8X4 = mybir.dt.float8_e4m3fn_x4
+ALU = mybir.AluOpType
+ACT = mybir.ActivationFunctionType
+
+P = 128
+PACK = 4
+T = 2048
+S = 512
+MEMBERS = 4
+BLOCK = 128
+N_BLOCKS = S // BLOCK
+EARLY = S - BLOCK
+HALF = S // 2
+Y_WINDOW = 2 * S + 1
+ROW_WINDOW = S + 17
+
+FLOPS = 4 * 2 * 512 * 512 * 512
+
+
+def tile_picked_tricdgxbmaxbegc_none_po_kernel(
+    tc, x_words, x_scales, w1_words, w1_scales, sl, th, gs, sl2, th2,
+    offs, n1, ca, cb, cd, n2, n3, n4, n5, out_0, out_1, out_2,
+):
+    nc = tc.nc
+    with ExitStack() as ctx:
+        lists = ctx.enter_context(tc.tile_pool(name="lists", bufs=1))
+        keep = ctx.enter_context(tc.tile_pool(name="keep", bufs=1))
+        psum = ctx.enter_context(tc.psum_pool(name="psum", bufs=8))
+
+        def load_list(name, src):
+            tile = lists.tile(list(src.shape), U16, name=name)
+            nc.sync.dma_start(tile[:], src)
+            return tile
+
+        def load_rows(name, src, queue):
+            tile = keep.tile([P, PACK], F32, name=name)
+            queue.dma_start(tile[:], src.rearrange("(p t) o -> p (t o)", t=PACK))
+            return tile
+
+        def load_words(name, src):
+            tile = keep.tile([P, src.shape[2]], U32, name=name, align_bytes=64)
+            nc.sync.dma_start(tile[:].bitcast(I32), src[0].rearrange("p n r -> p (n r)").bitcast(I32))
+            return tile
+
+        def zeroed_plane(name, width):
+            tile = keep.tile([P, width], U8, name=name, align_bytes=64)
+            nc.gpsimd.memset(tile[:].bitcast(I32), 0)
+            return tile
+
+        def load_scale_rows(tile, src, quad, queue):
+            queue.dma_start(
+                tile[32 * quad : 32 * quad + 4, :].bitcast(I32),
+                src[0, 4 * quad : 4 * quad + 4, :].bitcast(I32),
+            )
+
+        xs = zeroed_plane("xs", T)
+        w1s_raw = zeroed_plane("w1s_raw", S)
+        offs_sb = load_list("offs_sb", offs)
+        sl_sb = load_rows("sl_sb", sl, nc.sync)
+        th_sb = load_rows("th_sb", th, nc.sync)
+        xw = load_words("xw", x_words)
+        for quad in range(4):
+            load_scale_rows(xs, x_scales, quad, nc.scalar)
+        w1w_raw = load_words("w1w_raw", w1_words)
+        for quad in range(4):
+            load_scale_rows(w1s_raw, w1_scales, quad, nc.sync)
+        n1_sb = load_list("n1_sb", n1)
+        ca_sb = load_list("ca_sb", ca)
+        cb_sb = load_list("cb_sb", cb)
+        cd_sb = load_list("cd_sb", cd)
+        gs_sb = load_rows("gs_sb", gs, nc.sync)
+        sl2_sb = load_rows("sl2_sb", sl2, nc.sync)
+        th2_sb = load_rows("th2_sb", th2, nc.sync)
+        n2_sb = load_list("n2_sb", n2)
+        n3_sb = load_list("n3_sb", n3)
+        n5_sb = load_list("n5_sb", n5)
+        n4_sb = load_list("n4_sb", n4)
+
+        y = [keep.tile([P, Y_WINDOW], F32, name=f"y{t}") for t in range(PACK)]
+        for t in range(PACK):
+            nc.vector.memset(y[t][:, S:], 0.0)
+        q_rows = [keep.tile([P, ROW_WINDOW], F32, name=f"q_rows{t}") for t in range(PACK)]
+        m1 = [keep.tile([P, ROW_WINDOW], F32, name=f"m1_{t}") for t in range(PACK)]
+        for tile in q_rows + m1:
+            nc.vector.memset(tile[:, S:], 0.0)
+        out_scales = keep.tile([P, S], U8, name="out_scales", align_bytes=64)
+
+        def dealt(tile):
+            return tile[:].rearrange("p (t m) -> p m t", t=PACK)
+
+        def gather(name, table, offsets, dtype, deal):
+            tile = keep.tile([P, S], dtype, name=name, align_bytes=64)
+            nc.vector.tensor_copy(dealt(tile) if deal else tile[:], table[:].indirect(offsets[:]))
+            return tile
+
+        xq_s = gather("xq_s", xs, offs_sb, U8, False)
+        w1s = keep.tile([P, S], U8, name="w1s", align_bytes=64)
+        w1w = keep.tile([P, S], U32, name="w1w", align_bytes=64)
+        nc.scalar.copy(dealt(w1w), w1w_raw[:].rearrange("p (m t) -> p m t", t=PACK))
+        nc.vector.tensor_copy(dealt(w1s), w1s_raw[:].rearrange("p (m t) -> p m t", t=PACK))
+        xq_w = gather("xq_w", xw, offs_sb, U32, False)
+        bias1 = keep.tile([P, PACK], F32, name="bias1")
+        nc.vector.scalar_tensor_tensor(bias1[:], sl_sb[:], -1.0, th_sb[:], ALU.mult, ALU.mult)
+
+        def product(out, lhs_w, lhs_s, t, rhs_w, rhs_s, cols):
+            rows = slice(P * t, P * (t + 1))
+            nc.tensor.matmul_mx(
+                out, lhsT=lhs_w[:, rows].bitcast(FP8X4), lhsT_scale=lhs_s[:, rows],
+                rhs=rhs_w[:, cols].bitcast(FP8X4), rhs_scale=rhs_s[:, cols], start=True, stop=True,
+            )
+
+        for t in range(PACK):
+            acc = psum.tile([P, S], F32, name="acc")
+            product(acc[:], w1w, w1s, t, xq_w, xq_s, slice(0, S))
+            if t == 0:
+                nc.scalar.copy(y[t][:, :S], acc[:])
+            else:
+                nc.vector.tensor_copy(y[t][:, :S], acc[:])
+
+        entries = BLOCK * MEMBERS
+        sg = [keep.tile([P, PACK, entries], F32, name=f"sg{b}") for b in range(N_BLOCKS)]
+        for b in range(N_BLOCKS):
+            cols = slice(b * entries // 16, (b + 1) * entries // 16)
+            for t in range(PACK):
+                nc.scalar.activation(
+                    sg[b][:, t, :], y[t][:].indirect(n1_sb[:, cols]), ACT.Sigmoid,
+                    bias=bias1[:, t : t + 1], scale=sl_sb[:, t : t + 1],
+                )
+
+        z_w = keep.tile([P, S], U32, name="z_w", align_bytes=64)
+        z_s = keep.tile([P, S], U8, name="z_s", align_bytes=64)
+
+        def make_z(b, groups):
+            cols = slice(b * BLOCK, (b + 1) * BLOCK)
+            pairs = keep.tile([P, PACK, BLOCK, 2], F32, name=f"pairs{b}")
+            cnt = keep.tile([P, PACK, BLOCK], F32, name=f"cnt{b}")
+            larger = keep.tile([P, PACK, BLOCK], F32, name=f"larger{b}")
+            z_rows = keep.tile([P, PACK, BLOCK], BF16, name=f"z_rows{b}")
+            z_in = keep.tile([P, BLOCK, PACK], BF16, name=f"z_in{b}", align_bytes=64)
+            members = sg[b][:].rearrange("p t (j m) -> p t j m", m=MEMBERS)
+            for ts in groups:
+                nc.vector.tensor_tensor(pairs[:, ts], members[:, ts, :, 0:2], members[:, ts, :, 2:4], ALU.add)
+            for ts in groups:
+                nc.vector.tensor_tensor(cnt[:, ts], pairs[:, ts, :, 0], pairs[:, ts, :, 1], ALU.add)
+            for t in range(PACK):
+                nc.vector.scalar_tensor_tensor(larger[:, t, :], cnt[:, t, :], -1.5, y[t][:, cols], ALU.add, ALU.max)
+            for t in range(PACK):
+                nc.vector.tensor_scalar(z_rows[:, t, :], larger[:, t, :], gs_sb[:, t : t + 1], None, ALU.mult)
+            nc.vector.tensor_copy(z_in[:], z_rows[:].rearrange("p t j -> p j t"))
+            nc.vector.quantize_mx(
+                out=z_w[:, cols].bitcast(FP8X4), scales=z_s[:, cols], in_=z_in[:].rearrange("p j t -> p (j t)"),
+            )
+
+        halves = [slice(0, 2), slice(2, 4)]
+        ca_s = gather("ca_s", xs, ca_sb, U8, True)
+        ca_w = gather("ca_w", xw, ca_sb, U32, True)
+        cb_s = gather("cb_s", xs, cb_sb, U8, True)
+        make_z(0, halves)
+        cb_w = gather("cb_w", xw, cb_sb, U32, True)
+        make_z(1, halves)
+        cd_s = gather("cd_s", xs, cd_sb, U8, True)
+        cd_w = gather("cd_w", xw, cd_sb, U32, True)
+        make_z(2, halves)
+        bias2 = keep.tile([P, PACK], F32, name="bias2")
+        nc.vector.scalar_tensor_tensor(bias2[:], sl2_sb[:], -1.0, th2_sb[:], ALU.mult, ALU.mult)
+        make_z(3, [slice(0, 3), slice(3, 4)])
+
+        b_rows = y
+        h_rows = [keep.tile([P, S], F32, name=f"h_rows{t}") for t in range(PACK)]
+
+        def leave(engine, out, acc, factor):
+            if engine is nc.scalar:
+                nc.scalar.activation(out, acc, ACT.Copy, scale=factor)
+            else:
+                nc.vector.tensor_scalar(out, acc, factor, None, ALU.mult)
+
+        def early(lhs_w, lhs_s, rows, factor, engine):
+            for t in range(PACK):
+                acc = psum.tile([P, S], F32, name="acc")
+                product(acc[:, 0:256], lhs_w, lhs_s, t, z_w, z_s, slice(0, 256))
+                product(acc[:, 256:EARLY], lhs_w, lhs_s, t, z_w, z_s, slice(256, EARLY))
+                leave(engine, rows[t][:, :EARLY], acc[:, :EARLY], factor)
+
+        def late(lhs_w, lhs_s, rows, factor, engine):
+            acc = psum.tile([P, S], F32, name="acc")
+            for t in range(PACK):
+                product(acc[:, t * BLOCK : (t + 1) * BLOCK], lhs_w, lhs_s, t, z_w, z_s, slice(EARLY, S))
+            for t in range(PACK):
+                leave(engine, rows[t][:, EARLY:S], acc[:, t * BLOCK : (t + 1) * BLOCK], factor)
+
+        early(cb_w, cb_s, b_rows, 0.0625, nc.scalar)
+        early(ca_w, ca_s, h_rows, -0.03125, nc.scalar)
+        late(cb_w, cb_s, b_rows, 0.0625, nc.scalar)
+        late(ca_w, ca_s, h_rows, -0.03125, nc.vector)
+
+        def half_list(tile, h):
+            return tile[:, h * HALF // 16 : (h + 1) * HALF // 16]
+
+        sg2 = keep.tile([P, PACK, S], F32, name="sg2")
+        gated = keep.tile([P, PACK, S], F32, name="gated")
+        for t in range(PACK):
+            nc.scalar.activation(
+                sg2[:, t, :], b_rows[t][:].indirect(n2_sb[:]), ACT.Sigmoid,
+                bias=bias2[:, t : t + 1], scale=sl2_sb[:, t : t + 1],
+            )
+        late(cd_w, cd_s, q_rows, 0.0625, nc.vector)
+        early(cd_w, cd_s, q_rows, 0.0625, nc.scalar)
+
+        out_rows = out_0.rearrange("(p t) j -> p t j", t=PACK)
+        out_words = keep.tile([P, S], U32, name="out_words", align_bytes=64)
+        words_dram = out_1[0].rearrange("p n r -> p (n r)").bitcast(I32)
+        q5 = keep.tile([P, PACK, S], F32, name="q5")
+        m14 = keep.tile([P, PACK, S], F32, name="m14")
+        upper = keep.tile([P, PACK, S], F32, name="upper")
+        lower = keep.tile([P, PACK, S], F32, name="lower")
+        result = keep.tile([P, PACK, S], F32, name="result")
+        col_halves = [slice(0, HALF), slice(HALF, S)]
+
+        def make_m1(t):
+            nc.vector.scalar_tensor_tensor(gated[:, t, :], h_rows[t][:], -2.0, sg2[:, t, :], ALU.mult, ALU.mult)
+            for h, cols in enumerate(col_halves):
+                nc.vector.tensor_tensor(
+                    m1[t][:, cols], h_rows[t][:].indirect(half_list(n3_sb, h)), gated[:, t, cols], ALU.add)
+
+        def fetch(t):
+            nc.scalar.activation(q5[:, t, :], q_rows[t][:].indirect(n5_sb[:]), ACT.Copy)
+            if t < PACK - 1:
+                nc.scalar.activation(m14[:, t, :], m1[t][:].indirect(n4_sb[:]), ACT.Copy)
+            else:
+                for h, cols in enumerate(col_halves):
+                    nc.scalar.activation(m14[:, t, cols], m1[t][:].indirect(half_list(n4_sb, h)), ACT.Copy)
+
+        def finish(t, cols):
+            nc.vector.tensor_tensor(upper[:, t, cols], m1[t][:, cols], q5[:, t, cols], ALU.max)
+            nc.vector.tensor_tensor(lower[:, t, cols], m14[:, t, cols], q_rows[t][:, cols], ALU.min)
+            nc.vector.tensor_tensor(result[:, t, cols], upper[:, t, cols], lower[:, t, cols], ALU.subtract)
+            nc.sync.dma_start(out_rows[:, t, cols], result[:, t, cols])
+
+        def planes(h):
+            cols = col_halves[h]
+            rounded = keep.tile([P, HALF, PACK], BF16, name=f"rounded{h}", align_bytes=64)
+            nc.vector.tensor_copy(rounded[:], result[:, :, cols].rearrange("p t j -> p j t"))
+            nc.vector.quantize_mx(
+                out=out_words[:, cols].bitcast(FP8X4), scales=out_scales[:, cols],
+                in_=rounded[:].rearrange("p j t -> p (j t)"),
+            )
+            nc.sync.dma_start(words_dram[:, cols], out_words[:, cols].bitcast(I32))
+
+        for t in range(PACK):
+            make_m1(t)
+        for t in range(PACK):
+            fetch(t)
+        for t in range(PACK - 1):
+            finish(t, slice(0, S))
+        for h in range(2):
+            finish(PACK - 1, col_halves[h])
+            planes(h)
+        for quad in range(4):
+            queue = nc.sync if quad % 2 == 0 else nc.scalar
+            queue.dma_start(
+                out_2[0, 4 * quad : 4 * quad + 4, :].bitcast(I32),
+                out_scales[32 * quad : 32 * quad + 4, :].bitcast(I32),
+            )

@@ -1,6 +1,7 @@
 from contextlib import ExitStack
 
 import concourse.mybir as mybir
+from concourse.masks import make_identity
 
 F32 = mybir.dt.float32
 BF16 = mybir.dt.bfloat16
@@ -19,10 +20,9 @@ S = 512
 MEMBERS = 4
 BLOCK = 128
 N_BLOCKS = S // BLOCK
-EARLY = S - BLOCK
 HALF = S // 2
-Y_WINDOW = 2 * S + 1
-ROW_WINDOW = S + 17
+WIDE_WINDOW = 2 * S
+ROW_WINDOW = S + 16
 
 FLOPS = 4 * 2 * 512 * 512 * 512
 
@@ -35,7 +35,7 @@ def tile_picked_tricdgxbmaxbegc_none_po_kernel(
     with ExitStack() as ctx:
         lists = ctx.enter_context(tc.tile_pool(name="lists", bufs=1))
         keep = ctx.enter_context(tc.tile_pool(name="keep", bufs=1))
-        psum = ctx.enter_context(tc.psum_pool(name="psum", bufs=8))
+        psum = ctx.enter_context(tc.psum_pool(name="psum", bufs=1))
 
         def load_list(name, src):
             tile = lists.tile(list(src.shape), U16, name=name)
@@ -53,7 +53,7 @@ def tile_picked_tricdgxbmaxbegc_none_po_kernel(
             return tile
 
         def zeroed_plane(name, width):
-            tile = keep.tile([P, width], U8, name=name, align_bytes=64)
+            tile = keep.tile([P, width], U8, name=name, tag=name, align_bytes=64)
             nc.gpsimd.memset(tile[:].bitcast(I32), 0)
             return tile
 
@@ -67,16 +67,15 @@ def tile_picked_tricdgxbmaxbegc_none_po_kernel(
         w1s_raw = zeroed_plane("w1s_raw", S)
         offs_sb = load_list("offs_sb", offs)
         sl_sb = load_rows("sl_sb", sl, nc.sync)
-        th_sb = load_rows("th_sb", th, nc.sync)
-        xw = load_words("xw", x_words)
         for quad in range(4):
-            load_scale_rows(xs, x_scales, quad, nc.scalar)
+            load_scale_rows(xs, x_scales, quad, nc.scalar if quad < 2 else nc.sync)
+        xw = load_words("xw", x_words)
         w1w_raw = load_words("w1w_raw", w1_words)
         for quad in range(4):
             load_scale_rows(w1s_raw, w1_scales, quad, nc.sync)
+        th_sb = load_rows("th_sb", th, nc.sync)
         n1_sb = load_list("n1_sb", n1)
         ca_sb = load_list("ca_sb", ca)
-        cb_sb = load_list("cb_sb", cb)
         cd_sb = load_list("cd_sb", cd)
         gs_sb = load_rows("gs_sb", gs, nc.sync)
         sl2_sb = load_rows("sl2_sb", sl2, nc.sync)
@@ -85,136 +84,198 @@ def tile_picked_tricdgxbmaxbegc_none_po_kernel(
         n3_sb = load_list("n3_sb", n3)
         n5_sb = load_list("n5_sb", n5)
         n4_sb = load_list("n4_sb", n4)
+        cb_sb = load_list("cb_sb", cb)
 
-        y = [keep.tile([P, Y_WINDOW], F32, name=f"y{t}") for t in range(PACK)]
+        y = [keep.tile([P, WIDE_WINDOW], F32, name=f"y{t}") for t in range(PACK)]
         for t in range(PACK):
             nc.vector.memset(y[t][:, S:], 0.0)
+        ident = keep.tile([P, P], F32, name="ident")
+        make_identity(nc, ident[:])
+        h_rows = [keep.tile([P, WIDE_WINDOW], F32, name=f"h_rows{t}") for t in range(PACK)]
         q_rows = [keep.tile([P, ROW_WINDOW], F32, name=f"q_rows{t}") for t in range(PACK)]
         m1 = [keep.tile([P, ROW_WINDOW], F32, name=f"m1_{t}") for t in range(PACK)]
-        for tile in q_rows + m1:
-            nc.vector.memset(tile[:, S:], 0.0)
+        for tile in h_rows + q_rows + m1:
+            nc.gpsimd.memset(tile[:, S:], 0.0)
         out_scales = keep.tile([P, S], U8, name="out_scales", align_bytes=64)
-
-        def dealt(tile):
-            return tile[:].rearrange("p (t m) -> p m t", t=PACK)
-
-        def gather(name, table, offsets, dtype, deal):
-            tile = keep.tile([P, S], dtype, name=name, align_bytes=64)
-            nc.vector.tensor_copy(dealt(tile) if deal else tile[:], table[:].indirect(offsets[:]))
-            return tile
-
-        xq_s = gather("xq_s", xs, offs_sb, U8, False)
-        w1s = keep.tile([P, S], U8, name="w1s", align_bytes=64)
-        w1w = keep.tile([P, S], U32, name="w1w", align_bytes=64)
-        nc.scalar.copy(dealt(w1w), w1w_raw[:].rearrange("p (m t) -> p m t", t=PACK))
-        nc.vector.tensor_copy(dealt(w1s), w1s_raw[:].rearrange("p (m t) -> p m t", t=PACK))
-        xq_w = gather("xq_w", xw, offs_sb, U32, False)
-        bias1 = keep.tile([P, PACK], F32, name="bias1")
-        nc.vector.scalar_tensor_tensor(bias1[:], sl_sb[:], -1.0, th_sb[:], ALU.mult, ALU.mult)
-
-        def product(out, lhs_w, lhs_s, t, rhs_w, rhs_s, cols):
-            rows = slice(P * t, P * (t + 1))
-            nc.tensor.matmul_mx(
-                out, lhsT=lhs_w[:, rows].bitcast(FP8X4), lhsT_scale=lhs_s[:, rows],
-                rhs=rhs_w[:, cols].bitcast(FP8X4), rhs_scale=rhs_s[:, cols], start=True, stop=True,
-            )
-
-        for t in range(PACK):
-            acc = psum.tile([P, S], F32, name="acc")
-            product(acc[:], w1w, w1s, t, xq_w, xq_s, slice(0, S))
-            if t == 0:
-                nc.scalar.copy(y[t][:, :S], acc[:])
-            else:
-                nc.vector.tensor_copy(y[t][:, :S], acc[:])
-
-        entries = BLOCK * MEMBERS
-        sg = [keep.tile([P, PACK, entries], F32, name=f"sg{b}") for b in range(N_BLOCKS)]
-        for b in range(N_BLOCKS):
-            cols = slice(b * entries // 16, (b + 1) * entries // 16)
-            for t in range(PACK):
-                nc.scalar.activation(
-                    sg[b][:, t, :], y[t][:].indirect(n1_sb[:, cols]), ACT.Sigmoid,
-                    bias=bias1[:, t : t + 1], scale=sl_sb[:, t : t + 1],
-                )
-
-        z_w = keep.tile([P, S], U32, name="z_w", align_bytes=64)
-        z_s = keep.tile([P, S], U8, name="z_s", align_bytes=64)
-
-        def make_z(b, groups):
-            cols = slice(b * BLOCK, (b + 1) * BLOCK)
-            pairs = keep.tile([P, PACK, BLOCK, 2], F32, name=f"pairs{b}")
-            cnt = keep.tile([P, PACK, BLOCK], F32, name=f"cnt{b}")
-            larger = keep.tile([P, PACK, BLOCK], F32, name=f"larger{b}")
-            z_rows = keep.tile([P, PACK, BLOCK], BF16, name=f"z_rows{b}")
-            z_in = keep.tile([P, BLOCK, PACK], BF16, name=f"z_in{b}", align_bytes=64)
-            members = sg[b][:].rearrange("p t (j m) -> p t j m", m=MEMBERS)
-            for ts in groups:
-                nc.vector.tensor_tensor(pairs[:, ts], members[:, ts, :, 0:2], members[:, ts, :, 2:4], ALU.add)
-            for ts in groups:
-                nc.vector.tensor_tensor(cnt[:, ts], pairs[:, ts, :, 0], pairs[:, ts, :, 1], ALU.add)
-            for t in range(PACK):
-                nc.vector.scalar_tensor_tensor(larger[:, t, :], cnt[:, t, :], -1.5, y[t][:, cols], ALU.add, ALU.max)
-            for t in range(PACK):
-                nc.vector.tensor_scalar(z_rows[:, t, :], larger[:, t, :], gs_sb[:, t : t + 1], None, ALU.mult)
-            nc.vector.tensor_copy(z_in[:], z_rows[:].rearrange("p t j -> p j t"))
-            nc.vector.quantize_mx(
-                out=z_w[:, cols].bitcast(FP8X4), scales=z_s[:, cols], in_=z_in[:].rearrange("p j t -> p (j t)"),
-            )
-
-        halves = [slice(0, 2), slice(2, 4)]
-        ca_s = gather("ca_s", xs, ca_sb, U8, True)
-        ca_w = gather("ca_w", xw, ca_sb, U32, True)
-        cb_s = gather("cb_s", xs, cb_sb, U8, True)
-        make_z(0, halves)
-        cb_w = gather("cb_w", xw, cb_sb, U32, True)
-        make_z(1, halves)
-        cd_s = gather("cd_s", xs, cd_sb, U8, True)
-        cd_w = gather("cd_w", xw, cd_sb, U32, True)
-        make_z(2, halves)
-        bias2 = keep.tile([P, PACK], F32, name="bias2")
-        nc.vector.scalar_tensor_tensor(bias2[:], sl2_sb[:], -1.0, th2_sb[:], ALU.mult, ALU.mult)
-        make_z(3, [slice(0, 3), slice(3, 4)])
-
-        b_rows = y
-        h_rows = [keep.tile([P, S], F32, name=f"h_rows{t}") for t in range(PACK)]
-
-        def leave(engine, out, acc, factor):
-            if engine is nc.scalar:
-                nc.scalar.activation(out, acc, ACT.Copy, scale=factor)
-            else:
-                nc.vector.tensor_scalar(out, acc, factor, None, ALU.mult)
-
-        def early(lhs_w, lhs_s, rows, factor, engine):
-            for t in range(PACK):
-                acc = psum.tile([P, S], F32, name="acc")
-                product(acc[:, 0:256], lhs_w, lhs_s, t, z_w, z_s, slice(0, 256))
-                product(acc[:, 256:EARLY], lhs_w, lhs_s, t, z_w, z_s, slice(256, EARLY))
-                leave(engine, rows[t][:, :EARLY], acc[:, :EARLY], factor)
-
-        def late(lhs_w, lhs_s, rows, factor, engine):
-            acc = psum.tile([P, S], F32, name="acc")
-            for t in range(PACK):
-                product(acc[:, t * BLOCK : (t + 1) * BLOCK], lhs_w, lhs_s, t, z_w, z_s, slice(EARLY, S))
-            for t in range(PACK):
-                leave(engine, rows[t][:, EARLY:S], acc[:, t * BLOCK : (t + 1) * BLOCK], factor)
-
-        early(cb_w, cb_s, b_rows, 0.0625, nc.scalar)
-        early(ca_w, ca_s, h_rows, -0.03125, nc.scalar)
-        late(cb_w, cb_s, b_rows, 0.0625, nc.scalar)
-        late(ca_w, ca_s, h_rows, -0.03125, nc.vector)
 
         def half_list(tile, h):
             return tile[:, h * HALF // 16 : (h + 1) * HALF // 16]
 
+        col_halves = [slice(0, HALF), slice(HALF, S)]
+
+        def dealt(tile):
+            return tile[:].rearrange("p (t m) -> p m t", t=PACK)
+
+        def gather(name, table, offsets, dtype, deal, tag=None):
+            tile = keep.tile([P, S], dtype, name=name, tag=tag or name, align_bytes=64)
+            nc.vector.tensor_copy(dealt(tile) if deal else tile[:], table[:].indirect(offsets[:]))
+            return tile
+
+        xq_s = gather("xq_s", xs, offs_sb, U8, False)
+        w1s = keep.tile([P, S], U8, name="w1s", tag="w1s", align_bytes=64)
+        w1w = keep.tile([P, S], U32, name="w1w", tag="w1w", align_bytes=64)
+        w1w_by_m = w1w_raw[:].rearrange("p (m t) -> p m t", t=PACK)
+        nc.scalar.copy(w1w[:, 0:P], w1w_by_m[:, :, 0])
+        nc.scalar.copy(dealt(w1w)[:, :, 1:PACK], w1w_by_m[:, :, 1:PACK])
+        xq_w = [
+            keep.tile([P, HALF], U32, name=f"xq_w{h}", tag=tag, align_bytes=64)
+            for h, tag in enumerate(["xq_w", "w1s_raw"])
+        ]
+        nc.vector.tensor_copy(xq_w[0][:], xw[:].indirect(half_list(offs_sb, 0)))
+        nc.vector.tensor_copy(
+            w1s[:].rearrange("p (t m) -> p t m", t=PACK), w1s_raw[:].rearrange("p (m t) -> p t m", t=PACK))
+        nc.vector.tensor_copy(xq_w[1][:], xw[:].indirect(half_list(offs_sb, 1)))
+        bias1 = keep.tile([P, PACK], F32, name="bias1")
+        nc.vector.scalar_tensor_tensor(bias1[:], sl_sb[:], -1.0, th_sb[:], ALU.mult, ALU.mult)
+
+        def product(out, lhs_w, lhs_s, t, rhs_w, rhs_s):
+            rows = slice(P * t, P * (t + 1))
+            nc.tensor.matmul_mx(
+                out, lhsT=lhs_w[:, rows].bitcast(FP8X4), lhsT_scale=lhs_s[:, rows],
+                rhs=rhs_w.bitcast(FP8X4), rhs_scale=rhs_s, start=True, stop=True,
+            )
+
+        def new_bank():
+            return psum.tile([P, S], F32, name="acc", bufs=4)
+
+        for h, cols in enumerate(col_halves):
+            acc = new_bank()
+            product(acc[:, cols], w1w, w1s, 0, xq_w[h][:], xq_s[:, cols])
+            nc.vector.tensor_copy(y[0][:, cols], acc[:, cols])
+        for t in range(1, PACK):
+            acc = new_bank()
+            for h, cols in enumerate(col_halves):
+                product(acc[:, cols], w1w, w1s, t, xq_w[h][:], xq_s[:, cols])
+            nc.vector.tensor_copy(y[t][:, :S], acc[:])
+
+        entries = BLOCK * MEMBERS
+        sg = [keep.tile([P, PACK, entries], F32, name=f"sg{b}") for b in range(N_BLOCKS)]
+        for b in range(N_BLOCKS):
+            for t in range(PACK):
+                pieces = 2 if (b, t) == (N_BLOCKS - 1, PACK - 1) else 1
+                width = entries // pieces
+                for i in range(pieces):
+                    first = b * entries + i * width
+                    nc.scalar.activation(
+                        sg[b][:, t, i * width : (i + 1) * width],
+                        y[t][:].indirect(n1_sb[:, first // 16 : (first + width) // 16]), ACT.Sigmoid,
+                        bias=bias1[:, t : t + 1], scale=sl_sb[:, t : t + 1],
+                    )
+
+        z_w = keep.tile([P, S], U32, name="z_w", align_bytes=64)
+        z_s = keep.tile([P, S], U8, name="z_s", align_bytes=64)
+        y_turned = [keep.tile([P, PACK, P], F32, name=f"y_turned{b}") for b in range(N_BLOCKS)]
+        larger = [keep.tile([P, PACK, P], F32, name=f"larger{b}") for b in range(N_BLOCKS)]
+        z_in = [keep.tile([P, BLOCK, PACK], BF16, name=f"z_in{b}", tag=f"z_in{b}", align_bytes=64) for b in range(N_BLOCKS)]
+
+        def block_cols(b):
+            return slice(b * BLOCK, (b + 1) * BLOCK)
+
+        def turn_y(b, tiles=PACK):
+            acc = new_bank()
+            for t in range(tiles):
+                nc.tensor.transpose(acc[:, t * P : (t + 1) * P], y[t][:, block_cols(b)], ident[:])
+            nc.vector.tensor_copy(y_turned[b][:, :tiles, :].rearrange("j t p -> j (t p)"), acc[:, : tiles * P])
+
+        def count(b, first, tiles=2):
+            bank = psum.tile([P, 2, P], F32, name="cnt_bank", bufs=2)
+            for i in range(tiles):
+                for m in range(MEMBERS):
+                    nc.tensor.matmul(
+                        bank[:, i, :], lhsT=sg[b][:, first + i, m::MEMBERS], rhs=ident[:],
+                        is_transpose=True, start=(m == 0), stop=(m == MEMBERS - 1),
+                    )
+            ts = slice(first, first + tiles)
+            nc.vector.scalar_tensor_tensor(
+                larger[b][:, ts, :], bank[:, :tiles, :], -1.5, y_turned[b][:, ts, :], ALU.add, ALU.max)
+
+        def weigh(b, tiles=PACK):
+            bank = psum.tile([P, PACK, BLOCK], F32, name="back_bank", bufs=2)
+            for t in range(tiles):
+                nc.tensor.transpose(bank[:, t, :], larger[b][:, t, :], ident[:])
+            nc.vector.tensor_tensor(
+                z_in[b][:, :, :tiles], bank[:, :tiles, :].rearrange("p t j -> p j t"),
+                gs_sb[:, :tiles].unsqueeze(1).to_broadcast([P, BLOCK, tiles]), ALU.mult,
+            )
+
+        def direct(b, t, pieces):
+            cnt = keep.tile([P, BLOCK], F32, name="cnt", tag="z_in2", align_bytes=64)
+            width = BLOCK // pieces
+            members = sg[b][:, t, :].rearrange("p (j m) -> p j m", m=MEMBERS)
+            for i in range(pieces):
+                cols = slice(i * width, (i + 1) * width)
+                nc.vector.tensor_reduce(cnt[:, cols], members[:, cols, :], mybir.AxisListType.X, ALU.add)
+            nc.vector.scalar_tensor_tensor(larger[b][:, t, :], cnt[:], -1.5, y[t][:, block_cols(b)], ALU.add, ALU.max)
+            nc.vector.tensor_scalar(z_in[b][:, :, t], larger[b][:, t, :], gs_sb[:, t : t + 1], None, ALU.mult)
+
+        def quantise_z(b):
+            nc.vector.quantize_mx(
+                out=z_w[:, block_cols(b)].bitcast(FP8X4), scales=z_s[:, block_cols(b)],
+                in_=z_in[b][:].rearrange("p j t -> p (j t)"),
+            )
+
+        b_rows = y
+
+        def score(lhs_w, lhs_s, rows, factor, cols, engine):
+            width = cols.stop - cols.start
+            for first in range(0, PACK, S // width):
+                acc = new_bank()
+                tiles = range(first, first + S // width)
+                for i, t in enumerate(tiles):
+                    product(acc[:, i * width : (i + 1) * width], lhs_w, lhs_s, t, z_w[:, cols], z_s[:, cols])
+                for i, t in enumerate(tiles):
+                    piece = acc[:, i * width : (i + 1) * width]
+                    if engine is nc.scalar:
+                        nc.scalar.activation(rows[t][:, cols], piece, ACT.Copy, scale=factor)
+                    else:
+                        nc.vector.tensor_scalar(rows[t][:, cols], piece, factor, None, ALU.mult)
+
+        ca_s = gather("ca_s", xs, ca_sb, U8, True, "xq_s")
+        turn_y(0)
+        count(0, 0)
+        ca_w = gather("ca_w", xw, ca_sb, U32, True, "xq_w")
+        turn_y(1)
+        count(0, 2)
+        cd_s = gather("cd_s", xs, cd_sb, U8, True, "w1s")
+        turn_y(2)
+        count(1, 0)
+        weigh(0)
+        cd_w = gather("cd_w", xw, cd_sb, U32, True, "w1w")
+        quantise_z(0)
+        count(1, 2)
+        turn_y(3, 3)
+        cb_s = gather("cb_s", xs, cb_sb, U8, True)
+        count(2, 0)
+        weigh(1)
+        bias2 = keep.tile([P, PACK], F32, name="bias2")
+        nc.vector.scalar_tensor_tensor(bias2[:], sl2_sb[:], -1.0, th2_sb[:], ALU.mult, ALU.mult)
+        quantise_z(1)
+        cb_w = gather("cb_w", xw, cb_sb, U32, True)
+        count(2, 2)
+        score(cd_w, cd_s, q_rows, 0.0625, slice(0, HALF), nc.vector)
+        count(3, 0)
+        weigh(2)
+        quantise_z(2)
+        score(cb_w, cb_s, b_rows, 0.0625, col_halves[0], nc.scalar)
+        score(ca_w, ca_s, h_rows, -0.03125, col_halves[0], nc.scalar)
+        count(3, 2, 1)
+        weigh(3, 3)
+        score(cb_w, cb_s, b_rows, 0.0625, block_cols(2), nc.scalar)
+        direct(3, 3, 2)
+        quantise_z(3)
+        score(cb_w, cb_s, b_rows, 0.0625, block_cols(3), nc.scalar)
+        score(ca_w, ca_s, h_rows, -0.03125, col_halves[1], nc.vector)
+        score(cd_w, cd_s, q_rows, 0.0625, col_halves[1], nc.vector)
+
         sg2 = keep.tile([P, PACK, S], F32, name="sg2")
         gated = keep.tile([P, PACK, S], F32, name="gated")
+        h3 = keep.tile([P, S], F32, name="h3")
         for t in range(PACK):
             nc.scalar.activation(
                 sg2[:, t, :], b_rows[t][:].indirect(n2_sb[:]), ACT.Sigmoid,
                 bias=bias2[:, t : t + 1], scale=sl2_sb[:, t : t + 1],
             )
-        late(cd_w, cd_s, q_rows, 0.0625, nc.vector)
-        early(cd_w, cd_s, q_rows, 0.0625, nc.scalar)
+        nc.scalar.activation(h3[:], h_rows[PACK - 1][:].indirect(n3_sb[:]), ACT.Copy)
 
         out_rows = out_0.rearrange("(p t) j -> p t j", t=PACK)
         out_words = keep.tile([P, S], U32, name="out_words", align_bytes=64)
@@ -224,13 +285,13 @@ def tile_picked_tricdgxbmaxbegc_none_po_kernel(
         upper = keep.tile([P, PACK, S], F32, name="upper")
         lower = keep.tile([P, PACK, S], F32, name="lower")
         result = keep.tile([P, PACK, S], F32, name="result")
-        col_halves = [slice(0, HALF), slice(HALF, S)]
 
         def make_m1(t):
-            nc.vector.scalar_tensor_tensor(gated[:, t, :], h_rows[t][:], -2.0, sg2[:, t, :], ALU.mult, ALU.mult)
-            for h, cols in enumerate(col_halves):
-                nc.vector.tensor_tensor(
-                    m1[t][:, cols], h_rows[t][:].indirect(half_list(n3_sb, h)), gated[:, t, cols], ALU.add)
+            nc.vector.scalar_tensor_tensor(gated[:, t, :], h_rows[t][:, :S], -2.0, sg2[:, t, :], ALU.mult, ALU.mult)
+            if t < PACK - 1:
+                nc.vector.tensor_tensor(m1[t][:, :S], h_rows[t][:].indirect(n3_sb[:]), gated[:, t, :], ALU.add)
+            else:
+                nc.vector.tensor_tensor(m1[t][:, :S], h3[:], gated[:, t, :], ALU.add)
 
         def fetch(t):
             nc.scalar.activation(q5[:, t, :], q_rows[t][:].indirect(n5_sb[:]), ACT.Copy)
@@ -249,7 +310,10 @@ def tile_picked_tricdgxbmaxbegc_none_po_kernel(
         def planes(h):
             cols = col_halves[h]
             rounded = keep.tile([P, HALF, PACK], BF16, name=f"rounded{h}", align_bytes=64)
-            nc.vector.tensor_copy(rounded[:], result[:, :, cols].rearrange("p t j -> p j t"))
+            if h == 0:
+                nc.scalar.copy(rounded[:], result[:, :, cols].rearrange("p t j -> p j t"))
+            else:
+                nc.vector.tensor_copy(rounded[:], result[:, :, cols].rearrange("p t j -> p j t"))
             nc.vector.quantize_mx(
                 out=out_words[:, cols].bitcast(FP8X4), scales=out_scales[:, cols],
                 in_=rounded[:].rearrange("p j t -> p (j t)"),

@@ -78,13 +78,13 @@ def tile_picked_tricdgxbmaxbegc_none_po_kernel(
         ca_sb = load_list("ca_sb", ca)
         cd_sb = load_list("cd_sb", cd)
         gs_sb = load_rows("gs_sb", gs, nc.sync)
+        cb_sb = load_list("cb_sb", cb)
         sl2_sb = load_rows("sl2_sb", sl2, nc.sync)
         th2_sb = load_rows("th2_sb", th2, nc.sync)
         n2_sb = load_list("n2_sb", n2)
         n3_sb = load_list("n3_sb", n3)
         n5_sb = load_list("n5_sb", n5)
         n4_sb = load_list("n4_sb", n4)
-        cb_sb = load_list("cb_sb", cb)
 
         y = [keep.tile([P, WIDE_WINDOW], F32, name=f"y{t}") for t in range(PACK)]
         for t in range(PACK):
@@ -92,9 +92,11 @@ def tile_picked_tricdgxbmaxbegc_none_po_kernel(
         ident = keep.tile([P, P], F32, name="ident")
         make_identity(nc, ident[:])
         h_rows = [keep.tile([P, WIDE_WINDOW], F32, name=f"h_rows{t}") for t in range(PACK)]
-        q_rows = [keep.tile([P, ROW_WINDOW], F32, name=f"q_rows{t}") for t in range(PACK)]
+        q_all = keep.tile([P, (PACK + 1) * S], F32, name="q_all")
+        nc.gpsimd.memset(q_all[:, PACK * S :], 0.0)
+        q_rows = q_all[:].rearrange("p (t j) -> p t j", j=S)
         m1 = [keep.tile([P, ROW_WINDOW], F32, name=f"m1_{t}") for t in range(PACK)]
-        for tile in h_rows + q_rows + m1:
+        for tile in h_rows + m1:
             nc.gpsimd.memset(tile[:, S:], 0.0)
         out_scales = keep.tile([P, S], U8, name="out_scales", align_bytes=64)
 
@@ -216,19 +218,31 @@ def tile_picked_tricdgxbmaxbegc_none_po_kernel(
 
         b_rows = y
 
-        def score(lhs_w, lhs_s, rows, factor, cols, engine):
+        def leave(engine, out, piece, factor):
+            if engine is nc.scalar:
+                nc.scalar.activation(out, piece, ACT.Copy, scale=factor)
+            else:
+                nc.vector.tensor_scalar(out, piece, factor, None, ALU.mult)
+
+        def banks_of(lhs_w, lhs_s, cols, tiles):
             width = cols.stop - cols.start
-            for first in range(0, PACK, S // width):
-                acc = new_bank()
-                tiles = range(first, first + S // width)
-                for i, t in enumerate(tiles):
-                    product(acc[:, i * width : (i + 1) * width], lhs_w, lhs_s, t, z_w[:, cols], z_s[:, cols])
-                for i, t in enumerate(tiles):
-                    piece = acc[:, i * width : (i + 1) * width]
-                    if engine is nc.scalar:
-                        nc.scalar.activation(rows[t][:, cols], piece, ACT.Copy, scale=factor)
-                    else:
-                        nc.vector.tensor_scalar(rows[t][:, cols], piece, factor, None, ALU.mult)
+            filled = []
+            for first in range(0, len(tiles), S // width):
+                group = tiles[first : first + S // width]
+                acc = new_bank()[:, : len(group) * width].rearrange("p (i j) -> p i j", j=width)
+                for i, t in enumerate(group):
+                    product(acc[:, i, :], lhs_w, lhs_s, t, z_w[:, cols], z_s[:, cols])
+                filled.append((group, acc))
+            return filled
+
+        def score(lhs_w, lhs_s, rows, factor, cols, engine, tiles=range(PACK)):
+            for group, acc in banks_of(lhs_w, lhs_s, cols, tiles):
+                for i, t in enumerate(group):
+                    leave(engine, rows[t][:, cols], acc[:, i, :], factor)
+
+        def score_q(cols, engine):
+            for group, acc in banks_of(cd_w, cd_s, cols, range(PACK)):
+                leave(engine, q_rows[:, group.start : group.stop, cols], acc, 0.0625)
 
         ca_s = gather("ca_s", xs, ca_sb, U8, True, "xq_s")
         turn_y(0)
@@ -252,20 +266,23 @@ def tile_picked_tricdgxbmaxbegc_none_po_kernel(
         quantise_z(1)
         cb_w = gather("cb_w", xw, cb_sb, U32, True)
         count(2, 2)
-        score(cd_w, cd_s, q_rows, 0.0625, slice(0, HALF), nc.vector)
+        score_q(col_halves[0], nc.vector)
+        score(ca_w, ca_s, h_rows, -0.03125, col_halves[0], nc.vector)
         count(3, 0)
         weigh(2)
         quantise_z(2)
         score(cb_w, cb_s, b_rows, 0.0625, col_halves[0], nc.scalar)
-        score(ca_w, ca_s, h_rows, -0.03125, col_halves[0], nc.scalar)
         count(3, 2, 1)
         weigh(3, 3)
         score(cb_w, cb_s, b_rows, 0.0625, block_cols(2), nc.scalar)
+        score(ca_w, ca_s, h_rows, -0.03125, block_cols(2), nc.scalar)
+        score_q(block_cols(2), nc.scalar)
         direct(3, 3, 2)
         quantise_z(3)
-        score(cb_w, cb_s, b_rows, 0.0625, block_cols(3), nc.scalar)
-        score(ca_w, ca_s, h_rows, -0.03125, col_halves[1], nc.vector)
-        score(cd_w, cd_s, q_rows, 0.0625, col_halves[1], nc.vector)
+        score(cb_w, cb_s, b_rows, 0.0625, block_cols(3), nc.scalar, range(0, 1))
+        score(cb_w, cb_s, b_rows, 0.0625, block_cols(3), nc.vector, range(1, PACK))
+        score_q(block_cols(3), nc.vector)
+        score(ca_w, ca_s, h_rows, -0.03125, block_cols(3), nc.vector)
 
         sg2 = keep.tile([P, PACK, S], F32, name="sg2")
         gated = keep.tile([P, PACK, S], F32, name="gated")
@@ -293,17 +310,23 @@ def tile_picked_tricdgxbmaxbegc_none_po_kernel(
             else:
                 nc.vector.tensor_tensor(m1[t][:, :S], h3[:], gated[:, t, :], ALU.add)
 
+        def q_window(t):
+            return q_all[:, t * S : t * S + WIDE_WINDOW].indirect(n5_sb[:])
+
         def fetch(t):
-            nc.scalar.activation(q5[:, t, :], q_rows[t][:].indirect(n5_sb[:]), ACT.Copy)
+            if t > 0:
+                nc.scalar.activation(q5[:, t, :], q_window(t), ACT.Copy)
             if t < PACK - 1:
                 nc.scalar.activation(m14[:, t, :], m1[t][:].indirect(n4_sb[:]), ACT.Copy)
             else:
                 for h, cols in enumerate(col_halves):
                     nc.scalar.activation(m14[:, t, cols], m1[t][:].indirect(half_list(n4_sb, h)), ACT.Copy)
 
+        def take_upper(t):
+            nc.vector.tensor_tensor(upper[:, t, :], m1[t][:, :S], q5[:, t, :], ALU.max)
+
         def finish(t, cols):
-            nc.vector.tensor_tensor(upper[:, t, cols], m1[t][:, cols], q5[:, t, cols], ALU.max)
-            nc.vector.tensor_tensor(lower[:, t, cols], m14[:, t, cols], q_rows[t][:, cols], ALU.min)
+            nc.vector.tensor_tensor(lower[:, t, cols], m14[:, t, cols], q_rows[:, t, cols], ALU.min)
             nc.vector.tensor_tensor(result[:, t, cols], upper[:, t, cols], lower[:, t, cols], ALU.subtract)
             nc.sync.dma_start(out_rows[:, t, cols], result[:, t, cols])
 
@@ -320,14 +343,18 @@ def tile_picked_tricdgxbmaxbegc_none_po_kernel(
             )
             nc.sync.dma_start(words_dram[:, cols], out_words[:, cols].bitcast(I32))
 
+        nc.vector.tensor_copy(q5[:, 0, :], q_window(0))
         for t in range(PACK):
             make_m1(t)
         for t in range(PACK):
             fetch(t)
         for t in range(PACK - 1):
+            take_upper(t)
             finish(t, slice(0, S))
+        take_upper(PACK - 1)
         for h in range(2):
             finish(PACK - 1, col_halves[h])
+        for h in range(2):
             planes(h)
         for quad in range(4):
             queue = nc.sync if quad % 2 == 0 else nc.scalar

@@ -138,7 +138,7 @@ def tile_picked_tricdgxbmaxbegc_none_po_kernel(
             )
 
         def new_bank():
-            return psum.tile([P, S], F32, name="acc", bufs=4)
+            return psum.tile([P, S], F32, name="acc", bufs=5)
 
         for h, cols in enumerate(col_halves):
             acc = new_bank()
@@ -192,7 +192,7 @@ def tile_picked_tricdgxbmaxbegc_none_po_kernel(
                 larger[b][:, ts, :], bank[:, :tiles, :], -1.5, y_turned[b][:, ts, :], ALU.add, ALU.max)
 
         def weigh(b, tiles=PACK):
-            bank = psum.tile([P, PACK, BLOCK], F32, name="back_bank", bufs=2)
+            bank = psum.tile([P, PACK, BLOCK], F32, name="back_bank", bufs=1)
             for t in range(tiles):
                 nc.tensor.transpose(bank[:, t, :], larger[b][:, t, :], ident[:])
             nc.vector.tensor_tensor(
@@ -267,11 +267,11 @@ def tile_picked_tricdgxbmaxbegc_none_po_kernel(
         cb_w = gather("cb_w", xw, cb_sb, U32, True)
         count(2, 2)
         score_q(col_halves[0], nc.vector)
-        score(ca_w, ca_s, h_rows, -0.03125, col_halves[0], nc.vector)
         count(3, 0)
         weigh(2)
         quantise_z(2)
         score(cb_w, cb_s, b_rows, 0.0625, col_halves[0], nc.scalar)
+        score(ca_w, ca_s, h_rows, -0.03125, col_halves[0], nc.scalar)
         count(3, 2, 1)
         weigh(3, 3)
         score(cb_w, cb_s, b_rows, 0.0625, block_cols(2), nc.scalar)
@@ -286,13 +286,11 @@ def tile_picked_tricdgxbmaxbegc_none_po_kernel(
 
         sg2 = keep.tile([P, PACK, S], F32, name="sg2")
         gated = keep.tile([P, PACK, S], F32, name="gated")
-        h3 = keep.tile([P, S], F32, name="h3")
         for t in range(PACK):
             nc.scalar.activation(
                 sg2[:, t, :], b_rows[t][:].indirect(n2_sb[:]), ACT.Sigmoid,
                 bias=bias2[:, t : t + 1], scale=sl2_sb[:, t : t + 1],
             )
-        nc.scalar.activation(h3[:], h_rows[PACK - 1][:].indirect(n3_sb[:]), ACT.Copy)
 
         out_rows = out_0.rearrange("(p t) j -> p t j", t=PACK)
         out_words = keep.tile([P, S], U32, name="out_words", align_bytes=64)
@@ -305,10 +303,7 @@ def tile_picked_tricdgxbmaxbegc_none_po_kernel(
 
         def make_m1(t):
             nc.vector.scalar_tensor_tensor(gated[:, t, :], h_rows[t][:, :S], -2.0, sg2[:, t, :], ALU.mult, ALU.mult)
-            if t < PACK - 1:
-                nc.vector.tensor_tensor(m1[t][:, :S], h_rows[t][:].indirect(n3_sb[:]), gated[:, t, :], ALU.add)
-            else:
-                nc.vector.tensor_tensor(m1[t][:, :S], h3[:], gated[:, t, :], ALU.add)
+            nc.vector.tensor_tensor(m1[t][:, :S], h_rows[t][:].indirect(n3_sb[:]), gated[:, t, :], ALU.add)
 
         def q_window(t):
             return q_all[:, t * S : t * S + WIDE_WINDOW].indirect(n5_sb[:])

from contextlib import ExitStack

import concourse.mybir as mybir
from concourse.masks import make_identity

F32 = mybir.dt.float32
BF16 = mybir.dt.bfloat16
I32 = mybir.dt.int32
U32 = mybir.dt.uint32
U16 = mybir.dt.uint16
U8 = mybir.dt.uint8
FP8X4 = mybir.dt.float8_e4m3fn_x4
ALU = mybir.AluOpType
ACT = mybir.ActivationFunctionType

P = 128
PACK = 4
T = 2048
S = 512
MEMBERS = 4
BLOCK = 128
N_BLOCKS = S // BLOCK
HALF = S // 2
WIDE_WINDOW = 2 * S
ROW_WINDOW = S + 16

FLOPS = 4 * 2 * 512 * 512 * 512


def tile_picked_tricdgxbmaxbegc_none_po_kernel(
    tc, x_words, x_scales, w1_words, w1_scales, sl, th, gs, sl2, th2,
    offs, n1, ca, cb, cd, n2, n3, n4, n5, out_0, out_1, out_2,
):
    nc = tc.nc
    with ExitStack() as ctx:
        lists = ctx.enter_context(tc.tile_pool(name="lists", bufs=1))
        keep = ctx.enter_context(tc.tile_pool(name="keep", bufs=1))
        psum = ctx.enter_context(tc.psum_pool(name="psum", bufs=1))

        def load_list(name, src):
            tile = lists.tile(list(src.shape), U16, name=name)
            nc.sync.dma_start(tile[:], src)
            return tile

        def load_rows(name, src, queue):
            tile = keep.tile([P, PACK], F32, name=name)
            queue.dma_start(tile[:], src.rearrange("(p t) o -> p (t o)", t=PACK))
            return tile

        def load_words(name, src):
            tile = keep.tile([P, src.shape[2]], U32, name=name, align_bytes=64)
            nc.sync.dma_start(tile[:].bitcast(I32), src[0].rearrange("p n r -> p (n r)").bitcast(I32))
            return tile

        def zeroed_plane(name, width):
            tile = keep.tile([P, width], U8, name=name, tag=name, align_bytes=64)
            nc.gpsimd.memset(tile[:].bitcast(I32), 0)
            return tile

        def load_scale_rows(tile, src, quad, queue):
            queue.dma_start(
                tile[32 * quad : 32 * quad + 4, :].bitcast(I32),
                src[0, 4 * quad : 4 * quad + 4, :].bitcast(I32),
            )

        xs = zeroed_plane("xs", T)
        w1s_raw = zeroed_plane("w1s_raw", S)
        offs_sb = load_list("offs_sb", offs)
        sl_sb = load_rows("sl_sb", sl, nc.sync)
        for quad in range(4):
            load_scale_rows(xs, x_scales, quad, nc.scalar if quad < 2 else nc.sync)
        xw = load_words("xw", x_words)
        w1w_raw = load_words("w1w_raw", w1_words)
        for quad in range(4):
            load_scale_rows(w1s_raw, w1_scales, quad, nc.sync)
        th_sb = load_rows("th_sb", th, nc.sync)
        n1_sb = load_list("n1_sb", n1)
        ca_sb = load_list("ca_sb", ca)
        cd_sb = load_list("cd_sb", cd)
        gs_sb = load_rows("gs_sb", gs, nc.sync)
        cb_sb = load_list("cb_sb", cb)
        sl2_sb = load_rows("sl2_sb", sl2, nc.sync)
        th2_sb = load_rows("th2_sb", th2, nc.sync)
        n2_sb = load_list("n2_sb", n2)
        n3_sb = load_list("n3_sb", n3)
        n5_sb = load_list("n5_sb", n5)
        n4_sb = load_list("n4_sb", n4)

        y = [keep.tile([P, WIDE_WINDOW], F32, name=f"y{t}") for t in range(PACK)]
        for t in range(PACK):
            nc.vector.memset(y[t][:, S:], 0.0)
        ident = keep.tile([P, P], F32, name="ident")
        make_identity(nc, ident[:])
        h_rows = [keep.tile([P, WIDE_WINDOW], F32, name=f"h_rows{t}") for t in range(PACK)]
        q_all = keep.tile([P, (PACK + 1) * S], F32, name="q_all")
        nc.gpsimd.memset(q_all[:, PACK * S :], 0.0)
        q_rows = q_all[:].rearrange("p (t j) -> p t j", j=S)
        m1 = [keep.tile([P, ROW_WINDOW], F32, name=f"m1_{t}") for t in range(PACK)]
        for tile in h_rows + m1:
            nc.gpsimd.memset(tile[:, S:], 0.0)
        out_scales = keep.tile([P, S], U8, name="out_scales", align_bytes=64)

        def half_list(tile, h):
            return tile[:, h * HALF // 16 : (h + 1) * HALF // 16]

        col_halves = [slice(0, HALF), slice(HALF, S)]

        def dealt(tile):
            return tile[:].rearrange("p (t m) -> p m t", t=PACK)

        def gather(name, table, offsets, dtype, deal, tag=None):
            tile = keep.tile([P, S], dtype, name=name, tag=tag or name, align_bytes=64)
            nc.vector.tensor_copy(dealt(tile) if deal else tile[:], table[:].indirect(offsets[:]))
            return tile

        xq_s = gather("xq_s", xs, offs_sb, U8, False)
        w1s = keep.tile([P, S], U8, name="w1s", tag="w1s", align_bytes=64)
        w1w = keep.tile([P, S], U32, name="w1w", tag="w1w", align_bytes=64)
        w1w_by_m = w1w_raw[:].rearrange("p (m t) -> p m t", t=PACK)
        nc.scalar.copy(w1w[:, 0:P], w1w_by_m[:, :, 0])
        nc.scalar.copy(dealt(w1w)[:, :, 1:PACK], w1w_by_m[:, :, 1:PACK])
        xq_w = [
            keep.tile([P, HALF], U32, name=f"xq_w{h}", tag=tag, align_bytes=64)
            for h, tag in enumerate(["xq_w", "w1s_raw"])
        ]
        nc.vector.tensor_copy(xq_w[0][:], xw[:].indirect(half_list(offs_sb, 0)))
        nc.vector.tensor_copy(
            w1s[:].rearrange("p (t m) -> p t m", t=PACK), w1s_raw[:].rearrange("p (m t) -> p t m", t=PACK))
        nc.vector.tensor_copy(xq_w[1][:], xw[:].indirect(half_list(offs_sb, 1)))
        bias1 = keep.tile([P, PACK], F32, name="bias1")
        nc.vector.scalar_tensor_tensor(bias1[:], sl_sb[:], -1.0, th_sb[:], ALU.mult, ALU.mult)

        def product(out, lhs_w, lhs_s, t, rhs_w, rhs_s):
            rows = slice(P * t, P * (t + 1))
            nc.tensor.matmul_mx(
                out, lhsT=lhs_w[:, rows].bitcast(FP8X4), lhsT_scale=lhs_s[:, rows],
                rhs=rhs_w.bitcast(FP8X4), rhs_scale=rhs_s, start=True, stop=True,
            )

        def new_bank():
            return psum.tile([P, S], F32, name="acc", bufs=5)

        for h, cols in enumerate(col_halves):
            acc = new_bank()
            product(acc[:, cols], w1w, w1s, 0, xq_w[h][:], xq_s[:, cols])
            nc.vector.tensor_copy(y[0][:, cols], acc[:, cols])
        for t in range(1, PACK):
            acc = new_bank()
            for h, cols in enumerate(col_halves):
                product(acc[:, cols], w1w, w1s, t, xq_w[h][:], xq_s[:, cols])
            nc.vector.tensor_copy(y[t][:, :S], acc[:])

        entries = BLOCK * MEMBERS
        sg = [keep.tile([P, PACK, entries], F32, name=f"sg{b}") for b in range(N_BLOCKS)]
        for b in range(N_BLOCKS):
            for t in range(PACK):
                pieces = 2 if (b, t) == (N_BLOCKS - 1, PACK - 1) else 1
                width = entries // pieces
                for i in range(pieces):
                    first = b * entries + i * width
                    nc.scalar.activation(
                        sg[b][:, t, i * width : (i + 1) * width],
                        y[t][:].indirect(n1_sb[:, first // 16 : (first + width) // 16]), ACT.Sigmoid,
                        bias=bias1[:, t : t + 1], scale=sl_sb[:, t : t + 1],
                    )

        z_w = keep.tile([P, S], U32, name="z_w", align_bytes=64)
        z_s = keep.tile([P, S], U8, name="z_s", align_bytes=64)
        y_turned = [keep.tile([P, PACK, P], F32, name=f"y_turned{b}") for b in range(N_BLOCKS)]
        larger = [keep.tile([P, PACK, P], F32, name=f"larger{b}") for b in range(N_BLOCKS)]
        z_in = [keep.tile([P, BLOCK, PACK], BF16, name=f"z_in{b}", tag=f"z_in{b}", align_bytes=64) for b in range(N_BLOCKS)]

        def block_cols(b):
            return slice(b * BLOCK, (b + 1) * BLOCK)

        def turn_y(b, tiles=PACK):
            acc = new_bank()
            for t in range(tiles):
                nc.tensor.transpose(acc[:, t * P : (t + 1) * P], y[t][:, block_cols(b)], ident[:])
            nc.vector.tensor_copy(y_turned[b][:, :tiles, :].rearrange("j t p -> j (t p)"), acc[:, : tiles * P])

        def count(b, first, tiles=2):
            bank = psum.tile([P, 2, P], F32, name="cnt_bank", bufs=2)
            for i in range(tiles):
                for m in range(MEMBERS):
                    nc.tensor.matmul(
                        bank[:, i, :], lhsT=sg[b][:, first + i, m::MEMBERS], rhs=ident[:],
                        is_transpose=True, start=(m == 0), stop=(m == MEMBERS - 1),
                    )
            ts = slice(first, first + tiles)
            nc.vector.scalar_tensor_tensor(
                larger[b][:, ts, :], bank[:, :tiles, :], -1.5, y_turned[b][:, ts, :], ALU.add, ALU.max)

        def weigh(b, tiles=PACK):
            bank = psum.tile([P, PACK, BLOCK], F32, name="back_bank", bufs=1)
            for t in range(tiles):
                nc.tensor.transpose(bank[:, t, :], larger[b][:, t, :], ident[:])
            nc.vector.tensor_tensor(
                z_in[b][:, :, :tiles], bank[:, :tiles, :].rearrange("p t j -> p j t"),
                gs_sb[:, :tiles].unsqueeze(1).to_broadcast([P, BLOCK, tiles]), ALU.mult,
            )

        def direct(b, t, pieces):
            cnt = keep.tile([P, BLOCK], F32, name="cnt", tag="z_in2", align_bytes=64)
            width = BLOCK // pieces
            members = sg[b][:, t, :].rearrange("p (j m) -> p j m", m=MEMBERS)
            for i in range(pieces):
                cols = slice(i * width, (i + 1) * width)
                nc.vector.tensor_reduce(cnt[:, cols], members[:, cols, :], mybir.AxisListType.X, ALU.add)
            nc.vector.scalar_tensor_tensor(larger[b][:, t, :], cnt[:], -1.5, y[t][:, block_cols(b)], ALU.add, ALU.max)
            nc.vector.tensor_scalar(z_in[b][:, :, t], larger[b][:, t, :], gs_sb[:, t : t + 1], None, ALU.mult)

        def quantise_z(b):
            nc.vector.quantize_mx(
                out=z_w[:, block_cols(b)].bitcast(FP8X4), scales=z_s[:, block_cols(b)],
                in_=z_in[b][:].rearrange("p j t -> p (j t)"),
            )

        b_rows = y

        def leave(engine, out, piece, factor):
            if engine is nc.scalar:
                nc.scalar.activation(out, piece, ACT.Copy, scale=factor)
            else:
                nc.vector.tensor_scalar(out, piece, factor, None, ALU.mult)

        def banks_of(lhs_w, lhs_s, cols, tiles):
            width = cols.stop - cols.start
            filled = []
            for first in range(0, len(tiles), S // width):
                group = tiles[first : first + S // width]
                acc = new_bank()[:, : len(group) * width].rearrange("p (i j) -> p i j", j=width)
                for i, t in enumerate(group):
                    product(acc[:, i, :], lhs_w, lhs_s, t, z_w[:, cols], z_s[:, cols])
                filled.append((group, acc))
            return filled

        def score(lhs_w, lhs_s, rows, factor, cols, engine, tiles=range(PACK)):
            for group, acc in banks_of(lhs_w, lhs_s, cols, tiles):
                for i, t in enumerate(group):
                    leave(engine, rows[t][:, cols], acc[:, i, :], factor)

        def score_q(cols, engine):
            for group, acc in banks_of(cd_w, cd_s, cols, range(PACK)):
                leave(engine, q_rows[:, group.start : group.stop, cols], acc, 0.0625)

        ca_s = gather("ca_s", xs, ca_sb, U8, True, "xq_s")
        turn_y(0)
        count(0, 0)
        ca_w = gather("ca_w", xw, ca_sb, U32, True, "xq_w")
        turn_y(1)
        count(0, 2)
        cd_s = gather("cd_s", xs, cd_sb, U8, True, "w1s")
        turn_y(2)
        count(1, 0)
        weigh(0)
        cd_w = gather("cd_w", xw, cd_sb, U32, True, "w1w")
        quantise_z(0)
        count(1, 2)
        turn_y(3, 3)
        cb_s = gather("cb_s", xs, cb_sb, U8, True)
        count(2, 0)
        weigh(1)
        bias2 = keep.tile([P, PACK], F32, name="bias2")
        nc.vector.scalar_tensor_tensor(bias2[:], sl2_sb[:], -1.0, th2_sb[:], ALU.mult, ALU.mult)
        quantise_z(1)
        cb_w = gather("cb_w", xw, cb_sb, U32, True)
        count(2, 2)
        score_q(col_halves[0], nc.vector)
        count(3, 0)
        weigh(2)
        quantise_z(2)
        score(cb_w, cb_s, b_rows, 0.0625, col_halves[0], nc.scalar)
        score(ca_w, ca_s, h_rows, -0.03125, col_halves[0], nc.scalar)
        count(3, 2, 1)
        weigh(3, 3)
        score(cb_w, cb_s, b_rows, 0.0625, block_cols(2), nc.scalar)
        score(ca_w, ca_s, h_rows, -0.03125, block_cols(2), nc.scalar)
        score_q(block_cols(2), nc.scalar)
        direct(3, 3, 2)
        quantise_z(3)
        score(cb_w, cb_s, b_rows, 0.0625, block_cols(3), nc.scalar, range(0, 1))
        score(cb_w, cb_s, b_rows, 0.0625, block_cols(3), nc.vector, range(1, PACK))
        score_q(block_cols(3), nc.vector)
        score(ca_w, ca_s, h_rows, -0.03125, block_cols(3), nc.vector)

        sg2 = keep.tile([P, PACK, S], F32, name="sg2")
        gated = keep.tile([P, PACK, S], F32, name="gated")
        for t in range(PACK):
            nc.scalar.activation(
                sg2[:, t, :], b_rows[t][:].indirect(n2_sb[:]), ACT.Sigmoid,
                bias=bias2[:, t : t + 1], scale=sl2_sb[:, t : t + 1],
            )

        out_rows = out_0.rearrange("(p t) j -> p t j", t=PACK)
        out_words = keep.tile([P, S], U32, name="out_words", align_bytes=64)
        words_dram = out_1[0].rearrange("p n r -> p (n r)").bitcast(I32)
        q5 = keep.tile([P, PACK, S], F32, name="q5")
        m14 = keep.tile([P, PACK, S], F32, name="m14")
        upper = keep.tile([P, PACK, S], F32, name="upper")
        lower = keep.tile([P, PACK, S], F32, name="lower")
        result = keep.tile([P, PACK, S], F32, name="result")

        def make_m1(t):
            nc.vector.scalar_tensor_tensor(gated[:, t, :], h_rows[t][:, :S], -2.0, sg2[:, t, :], ALU.mult, ALU.mult)
            nc.vector.tensor_tensor(m1[t][:, :S], h_rows[t][:].indirect(n3_sb[:]), gated[:, t, :], ALU.add)

        def q_window(t):
            return q_all[:, t * S : t * S + WIDE_WINDOW].indirect(n5_sb[:])

        def fetch(t):
            if t > 0:
                nc.scalar.activation(q5[:, t, :], q_window(t), ACT.Copy)
            if t < PACK - 1:
                nc.scalar.activation(m14[:, t, :], m1[t][:].indirect(n4_sb[:]), ACT.Copy)
            else:
                for h, cols in enumerate(col_halves):
                    nc.scalar.activation(m14[:, t, cols], m1[t][:].indirect(half_list(n4_sb, h)), ACT.Copy)

        def take_upper(t):
            nc.vector.tensor_tensor(upper[:, t, :], m1[t][:, :S], q5[:, t, :], ALU.max)

        def finish(t, cols):
            nc.vector.tensor_tensor(lower[:, t, cols], m14[:, t, cols], q_rows[:, t, cols], ALU.min)
            nc.vector.tensor_tensor(result[:, t, cols], upper[:, t, cols], lower[:, t, cols], ALU.subtract)
            nc.sync.dma_start(out_rows[:, t, cols], result[:, t, cols])

        def planes(h):
            cols = col_halves[h]
            rounded = keep.tile([P, HALF, PACK], BF16, name=f"rounded{h}", align_bytes=64)
            if h == 0:
                nc.scalar.copy(rounded[:], result[:, :, cols].rearrange("p t j -> p j t"))
            else:
                nc.vector.tensor_copy(rounded[:], result[:, :, cols].rearrange("p t j -> p j t"))
            nc.vector.quantize_mx(
                out=out_words[:, cols].bitcast(FP8X4), scales=out_scales[:, cols],
                in_=rounded[:].rearrange("p j t -> p (j t)"),
            )
            nc.sync.dma_start(words_dram[:, cols], out_words[:, cols].bitcast(I32))

        nc.vector.tensor_copy(q5[:, 0, :], q_window(0))
        for t in range(PACK):
            make_m1(t)
        for t in range(PACK):
            fetch(t)
        for t in range(PACK - 1):
            take_upper(t)
            finish(t, slice(0, S))
        take_upper(PACK - 1)
        for h in range(2):
            finish(PACK - 1, col_halves[h])
        for h in range(2):
            planes(h)
        for quad in range(4):
            queue = nc.sync if quad % 2 == 0 else nc.scalar
            queue.dma_start(
                out_2[0, 4 * quad : 4 * quad + 4, :].bitcast(I32),
                out_scales[32 * quad : 32 * quad + 4, :].bitcast(I32),
            )
